import numpy as np
import ml_dtypes


def mxq(x, axis, fmt="e4m3"):
    dtype, down = {"e4m3": (ml_dtypes.float8_e4m3fn, 7), "e5m2": (ml_dtypes.float8_e5m2, 14)}[fmt]
    v = np.moveaxis(np.asarray(x, np.float32).astype(ml_dtypes.bfloat16).astype(np.float64), axis, -1)
    blocks = v.reshape(v.shape[:-1] + (-1, 32))
    amax = np.abs(blocks).max(-1, keepdims=True)
    byte = np.maximum(np.where(amax > 0, np.frexp(amax)[1] - 1 + 127, 0) - down, 1)
    scale = np.exp2(byte - 127.0)
    codes = (blocks / scale).astype(np.float32).astype(dtype).astype(np.float64)
    return np.moveaxis((codes * scale).reshape(v.shape), -1, axis)


WIDE = False


def mx_kscale(k):
    if not WIDE:
        return np.ones(k)
    levels = np.array([10, -10, 5, -5, 0])
    if k % 512:
        return np.exp2(np.random.permutation(np.resize(levels, k // 32))).repeat(32)
    a = np.empty((k // 512, 16))
    for p in range(k // 512):
        a[p, :8] = np.random.permutation(np.resize(levels, 8))
        for g in range(8):
            far = levels[np.abs(levels - a[p, g]) >= 10]
            a[p, g + 8] = far[np.random.randint(len(far))]
    return np.exp2(a.ravel()).repeat(32)


def f64(x):
    return np.asarray(x).astype(np.float64)


def striped(idx):
    return np.tile(np.asarray(idx).reshape(-1, 16).T, (8, 1)).astype(np.uint16)


def unstriped(offs):
    return offs[:16].T.reshape(-1).astype(np.int64)


def striped8(idx):
    return np.asarray(idx).reshape(8, -1, 16).transpose(0, 2, 1).reshape(128, -1).astype(np.uint16)


def unstriped8(offs):
    return offs.reshape(8, 16, -1).transpose(0, 2, 1).reshape(8, -1).astype(np.int64)


def pick8(x, idx, run):
    r = np.arange(len(x))
    return x[r[:, None], idx[r % (8 * run) // run]]


E2M1 = np.array([0.0, 0.5, 1.0, 1.5, 2.0, 3.0, 4.0, 6.0, -0.0, -0.5, -1.0, -1.5, -2.0, -3.0, -4.0, -6.0])


def pack_weight(w, fmt):
    k, n = w.shape
    w = f64(np.asarray(w, np.float32).astype(ml_dtypes.bfloat16)).reshape(k // 32, 32, n)
    amax = np.abs(w).max(1)
    if fmt == "e4m3":
        byte = np.frexp(amax)[1] - 1 + 127 - 7
    else:
        mant, ex = np.frexp(amax / 6.0)
        byte = np.where(mant > 0.5, ex, ex - 1) + 127
    byte = np.clip(np.where(amax > 0, byte, 1), 1, 254)
    scaled = (w * np.exp2(127.0 - byte)[:, None, :]).reshape(k, n).astype(np.float32)
    by_word = np.ascontiguousarray(scaled.reshape(k // 512, 128, 4, n).transpose(0, 1, 3, 2))
    if fmt == "e4m3":
        words = by_word.astype(ml_dtypes.float8_e4m3fn).view(np.uint8)
    else:
        c = by_word.astype(ml_dtypes.float4_e2m1fn).view(np.uint8) & 0xF
        words = (c[..., 0::2] | (c[..., 1::2] << 4)).reshape(k // 512, 128, 2 * n)
    return np.ascontiguousarray(words), np.ascontiguousarray(byte.astype(np.uint8).reshape(k // 512, 16, n))


def unpack_weight(words, scales, fmt):
    g, _, n = scales.shape
    words = np.ascontiguousarray(words).reshape(g, 128, n, -1)
    if fmt == "e4m3":
        vals = words.view(ml_dtypes.float8_e4m3fn).astype(np.float64)
    else:
        nib = np.empty((g, 128, n, 4), np.uint8)
        nib[..., 0::2] = words & 0xF
        nib[..., 1::2] = words >> 4
        vals = E2M1[nib]
    vals = vals * np.repeat(np.exp2(scales.astype(np.float64) - 127.0), 8, axis=1)[..., None]
    return vals.transpose(0, 1, 3, 2).reshape(g * 512, n)


K, J, R, T, C, O, N, S = 512, 256, 512, 1024, 512, 256, 256, 1024


def setup_inputs():
    n = np.random.standard_normal
    idx = np.random.permutation(T)[:J]
    idx2 = np.stack([np.random.permutation(C)[:J] for _ in range(8)])
    idx3 = np.stack([np.random.permutation(C)[:J] for _ in range(8)])
    idx4 = np.stack([np.random.permutation(C)[:O] for _ in range(8)])
    idx5 = np.random.permutation(S)[:N]
    fk = mx_kscale(K)
    fr = mx_kscale(R)
    xtp = pack_weight(n((K, T)) * fk[:, None], "e4m3")
    wp = pack_weight(n((K, R)) * 1 / np.sqrt(K) / fk[:, None] * fr, "e4m3")
    w2p = pack_weight(n((K, R)) * 1 / np.sqrt(K) / fk[:, None] * fr, "e2m1")
    vsp = pack_weight(n((R, S)) * 1 / np.sqrt(R) / fr[:, None], "e2m1")
    return {
        "xt_words": xtp[0],
        "xt_scales": xtp[1],
        "w_words": wp[0],
        "w_scales": wp[1],
        "w2_words": w2p[0],
        "w2_scales": w2p[1],
        "sa": (np.random.uniform(0.5, 1.6, (R, 1))).astype(np.float32),
        "vs_words": vsp[0],
        "vs_scales": vsp[1],
        "offs": striped(idx),
        "offs2": striped8(idx2),
        "offs3": striped8(idx3),
        "offs4": striped8(idx4),
        "offs5": striped(idx5),
    }


def reference(xt_words, xt_scales, w_words, w_scales, w2_words, w2_scales, sa, vs_words, vs_scales, offs, offs2, offs3, offs4, offs5):
    idx = unstriped(offs)
    idx2 = unstriped8(offs2)
    idx3 = unstriped8(offs3)
    idx4 = unstriped8(offs4)
    idx5 = unstriped(offs5)
    xtu = unpack_weight(xt_words, xt_scales, "e4m3")
    wu = unpack_weight(w_words, w_scales, "e4m3")
    w2u = unpack_weight(w2_words, w2_scales, "e2m1")
    vsu = unpack_weight(vs_words, vs_scales, "e2m1")
    xtidxg = xtu[:, idx]
    a = wu.T @ xtidxg
    b = w2u.T @ xtidxg
    pw = np.zeros((R, C))
    pw[np.arange(R)[:, None], idx2[np.arange(R) % 512 // 64]] = a
    pv = np.zeros((R, C))
    pv[np.arange(R)[:, None], idx3[np.arange(R) % 512 // 64]] = b
    pg = np.maximum(pw, pv)
    pm = np.mean(pg, axis=1, keepdims=True)
    g1 = np.maximum(pg - pm, 0.0)
    hid = pick8(g1, idx4, 64) * f64(sa)
    vsidx5g = vsu[:, idx5]
    hidq = mxq(hid, 0, "e4m3")
    y = vsidx5g.T @ hidq
    return y

@@ -1,0 +1,190 @@
+from contextlib import ExitStack
+
+import concourse.mybir as mybir
+
+K, J, R, T, C, O, N, S = 512, 256, 512, 1024, 512, 256, 256, 1024
+FLOPS = 2 * K * R * J * 2 + 2 * R * N * O
+
+F32 = mybir.dt.float32
+BF16 = mybir.dt.bfloat16
+I32 = mybir.dt.int32
+U32 = mybir.dt.uint32
+U16 = mybir.dt.uint16
+U8 = mybir.dt.uint8
+FP8X4 = mybir.dt.float8_e4m3fn_x4
+FP4X4 = mybir.dt.float4_e2m1fn_x4
+ALU = mybir.AluOpType
+COPY = mybir.ActivationFunctionType.Copy
+
+P = 128
+PACK = 4
+HALF = 128
+LIST_ROWS = 16
+
+
+def tile_picked_tokens_plain_twin_aboveaverage_store_plain_kernel(
+    tc, xt_words, xt_scales, w_words, w_scales, w2_words, w2_scales, sa, vs_words, vs_scales,
+    offs, offs2, offs3, offs4, offs5, out,
+):
+    nc = tc.nc
+    with ExitStack() as ctx:
+        keep = ctx.enter_context(tc.tile_pool(name="keep", bufs=1))
+        psum = ctx.enter_context(tc.psum_pool(name="psum", bufs=4))
+
+        def load_list(dram, name):
+            tile = keep.tile([P, J // LIST_ROWS], U16, name=name)
+            nc.sync.dma_start(tile[:], dram)
+            return tile
+
+        def entries(tile, first, count):
+            return tile[:, first // LIST_ROWS : (first + count) // LIST_ROWS]
+
+        def cleared_plane(width, name):
+            plane = keep.tile([P, width], U8, name=name, align_bytes=64)
+            nc.vector.memset(plane[:].bitcast(I32), 0)
+            return plane
+
+        def load_plane(queue, plane, scales):
+            for q in range(4):
+                queue.dma_start(plane[32 * q : 32 * q + 4, :].bitcast(I32), scales[0, 4 * q : 4 * q + 4, :].bitcast(I32))
+
+        def load_staged_scales(queue, scales, name):
+            staged = keep.tile([4, 4, R // 4], I32, name=name)
+            queue.dma_start(staged[:], scales[0].bitcast(I32).rearrange("(q i) n -> i q n", i=4))
+            return staged
+
+        def spread(plane, staged):
+            for q in range(4):
+                nc.vector.tensor_copy(plane[32 * q : 32 * q + 4, :].bitcast(I32), staged[:, q, :])
+
+        xt_plane = cleared_plane(T, "xt_plane")
+        tok_list = load_list(offs, "tok_list")
+        w2_staged = load_staged_scales(nc.scalar, w2_scales, "w2_staged")
+        load_plane(nc.scalar, xt_plane, xt_scales)
+        w2_raw = keep.tile([P, 2 * R], U8, name="w2_raw")
+        nc.sync.dma_start(w2_raw[:].bitcast(I32), w2_words[0].bitcast(I32))
+        xt_raw = keep.tile([P, T], U32, name="xt_raw")
+        nc.sync.dma_start(xt_raw[:].bitcast(I32), xt_words[0].rearrange("p n t -> p (n t)").bitcast(I32))
+        b_list = load_list(offs3, "b_list")
+        w_staged = load_staged_scales(nc.sync, w_scales, "w_staged")
+        w_raw = keep.tile([P, R], I32, name="w_raw")
+        nc.sync.dma_start(w_raw[:], w_words[0].rearrange("p n t -> p (n t)").bitcast(I32))
+        a_list = load_list(offs2, "a_list")
+        vs_list = load_list(offs5, "vs_list")
+        vs_raw = keep.tile([P, S], U16, name="vs_raw")
+        nc.sync.dma_start(vs_raw[:].bitcast(I32), vs_words[0].bitcast(I32))
+        w2_plane = cleared_plane(R, "w2_plane")
+        w_plane = cleared_plane(R, "w_plane")
+        boards_b = []
+        boards_a = []
+        for i in range(2):
+            boards_b.append(keep.tile([P, C], F32, name=f"board_b{i}"))
+            nc.vector.memset(boards_b[i][:], 0.0)
+            boards_a.append(keep.tile([P, C], F32, name=f"board_a{i}"))
+            nc.vector.memset(boards_a[i][:], 0.0)
+        vs_plane = cleared_plane(S, "vs_plane")
+        load_plane(nc.sync, vs_plane, vs_scales)
+        place_list = load_list(offs4, "place_list")
+        sa_sb = keep.tile([P, PACK], F32, name="sa_sb")
+        nc.sync.dma_start(sa_sb[:], sa.rearrange("(p t) one -> p (t one)", t=PACK))
+
+        def deal(raw, dtype, per_column, t0, t1, name):
+            dealt = keep.tile([P, t1 - t0, P * per_column], dtype, name=name, align_bytes=64)
+            nc.vector.tensor_copy(
+                dealt[:].rearrange("p t (m b) -> p t m b", b=per_column),
+                raw[:].rearrange("p (m t b) -> p t m b", t=PACK, b=per_column)[:, t0:t1, :, :],
+            )
+            return [dealt[:, t, :] for t in range(t1 - t0)]
+
+        xg_words = keep.tile([P, J], U32, name="xg_words", align_bytes=64)
+        xg_plane = keep.tile([P, J], U8, name="xg_plane", align_bytes=64)
+
+        def product_to_board(words, plane, board, board_list, first, count, name, tag):
+            acc = psum.tile([P, count], F32, name="acc")
+            nc.tensor.matmul_mx(
+                out=acc[:], lhsT=words, lhsT_scale=plane,
+                rhs=xg_words[:, first : first + count].bitcast(FP8X4), rhs_scale=xg_plane[:, first : first + count],
+                start=True, stop=True,
+            )
+            result = keep.tile([P, count], F32, name=name, tag=tag, align_bytes=64)
+            nc.vector.tensor_copy(result[:], acc[:])
+            nc.scalar.activation(board[:].indirect(entries(board_list, first, count)), result[:], COPY)
+
+        spread(w2_plane, w2_staged)
+        w2_plane_t = deal(w2_plane, U8, 1, 0, 1, "w2_plane_first")
+        w2_words_t = deal(w2_raw, U8, 2, 0, 1, "w2_words_first")
+        for first in range(0, J, HALF):
+            cols = slice(first, first + HALF)
+            nc.vector.tensor_copy(xg_plane[:, cols], xt_plane[:].indirect(entries(tok_list, first, HALF)))
+            nc.vector.tensor_copy(xg_words[:, cols], xt_raw[:].indirect(entries(tok_list, first, HALF)))
+            product_to_board(w2_words_t[0].bitcast(FP4X4), w2_plane_t[0], boards_b[0], b_list, first, HALF,
+                             f"b0_{first}", f"b0_{first}")
+        spread(w_plane, w_staged)
+        w_plane_t = deal(w_plane, U8, 1, 0, 1, "w_plane_first")
+        w_words_t = deal(w_raw, I32, 1, 0, 1, "w_words_first")
+        product_to_board(w_words_t[0].bitcast(FP8X4), w_plane_t[0], boards_a[0], a_list, 0, J, "a0", "a0")
+        w2_plane_t = w2_plane_t + deal(w2_plane, U8, 1, 1, PACK, "w2_plane_rest")
+        w2_words_t = w2_words_t + deal(w2_raw, U8, 2, 1, PACK, "w2_words_rest")
+        w_plane_t = w_plane_t + deal(w_plane, U8, 1, 1, PACK, "w_plane_rest")
+        w_words_t = w_words_t + deal(w_raw, I32, 1, 1, PACK, "w_words_rest")
+
+        vg_words = keep.tile([P, N], U16, name="vg_words", align_bytes=64)
+        vg_plane = keep.tile([P, N], U8, name="vg_plane", align_bytes=64)
+
+        g1 = []
+
+        def above_average(t):
+            pg = keep.tile([P, C], F32, name=f"pg{t}")
+            total = keep.tile([P, 1], F32, name=f"total{t}")
+            nc.vector.scalar_tensor_tensor(
+                out=pg[:], in0=boards_a[t % 2][:], scalar=1.0, in1=boards_b[t % 2][:],
+                op0=ALU.mult, op1=ALU.max, accum_out=total[:],
+            )
+            mean = keep.tile([P, 1], F32, name=f"mean{t}")
+            nc.vector.tensor_scalar(out=mean[:], in0=total[:], scalar1=1.0 / C, scalar2=None, op0=ALU.mult)
+            g = keep.tile([P, C], F32, name=f"g1_{t}")
+            nc.vector.tensor_scalar(out=g[:], in0=pg[:], scalar1=mean[:], scalar2=0.0, op0=ALU.subtract, op1=ALU.max)
+            g1.append(g)
+
+        for t in range(1, PACK):
+            product_to_board(w2_words_t[t].bitcast(FP4X4), w2_plane_t[t], boards_b[t % 2], b_list, 0, J, f"b{t}", f"b{t}")
+            product_to_board(w_words_t[t].bitcast(FP8X4), w_plane_t[t], boards_a[t % 2], a_list, 0, J, f"a{t}",
+                             "last" if t == PACK - 1 else f"a{t}")
+            if t == 1:
+                nc.vector.tensor_copy(vg_words[:], vs_raw[:].indirect(vs_list[:]))
+                nc.vector.tensor_copy(vg_plane[:], vs_plane[:].indirect(vs_list[:]))
+            above_average(t - 1)
+        above_average(PACK - 1)
+
+        hid = keep.tile([P, PACK, O], BF16, name="hid", tag="last", align_bytes=64)
+        for t in range(PACK - 1):
+            nc.scalar.activation(hid[:, t, :], g1[t][:].indirect(place_list[:]), COPY, scale=sa_sb[:, t : t + 1])
+        t = PACK - 1
+        for first in range(0, O, HALF):
+            nc.scalar.activation(hid[:, t, first : first + HALF], g1[t][:].indirect(entries(place_list, first, HALF)),
+                                 COPY, scale=sa_sb[:, t : t + 1])
+        grouped = []
+        for first in range(0, O, HALF):
+            tile = keep.tile([P, HALF, PACK], BF16, name=f"grouped{first}", align_bytes=64)
+            nc.vector.tensor_copy(tile[:], hid[:, :, first : first + HALF].rearrange("p t o -> p o t"))
+            grouped.append(tile)
+        out_view = out.rearrange("(b p) o -> p b o", p=P)
+        for h in range(2):
+            codes = keep.tile([P, HALF], U32, name=f"hid_words{h}", align_bytes=64)
+            plane = keep.tile([P, HALF], U8, name=f"hid_plane{h}", align_bytes=64)
+            nc.vector.quantize_mx(out=codes[:].bitcast(FP8X4), scales=plane[:],
+                                  in_=grouped[h][:].rearrange("p o t -> p (o t)"))
+            cols = slice(h * HALF, (h + 1) * HALF)
+            for b in range(2):
+                y = psum.tile([P, HALF], F32, name="y")
+                nc.tensor.matmul_mx(
+                    out=y[:], lhsT=vg_words[:, b * P : (b + 1) * P].bitcast(FP4X4), lhsT_scale=vg_plane[:, b * P : (b + 1) * P],
+                    rhs=codes[:].bitcast(FP8X4), rhs_scale=plane[:], start=True, stop=True,
+                )
+                y_sb = keep.tile([P, HALF], F32, name=f"y{h}{b}")
+                if h == 1 and b == 0:
+                    nc.vector.tensor_copy(y_sb[:], y[:])
+                else:
+                    nc.scalar.copy(y_sb[:], y[:])
+                queue = nc.scalar if h == 1 and b == 1 else nc.sync
+                queue.dma_start(out_view[:, b, cols], y_sb[:])

@@ -29,6 +29,7 @@ def tile_picked_tokens_plain_twin_aboveaverage_store_plain_kernel(
     nc = tc.nc
     with ExitStack() as ctx:
         keep = ctx.enter_context(tc.tile_pool(name="keep", bufs=1))
+        reuse = ctx.enter_context(tc.tile_pool(name="reuse", bufs=1))
         psum = ctx.enter_context(tc.psum_pool(name="psum", bufs=4))
 
         def load_list(dram, name):
@@ -39,17 +40,18 @@ def tile_picked_tokens_plain_twin_aboveaverage_store_plain_kernel(
         def entries(tile, first, count):
             return tile[:, first // LIST_ROWS : (first + count) // LIST_ROWS]
 
-        def cleared_plane(width, name):
-            plane = keep.tile([P, width], U8, name=name, align_bytes=64)
+        def placed(shape, dtype, name, offset):
+            if offset is None:
+                return keep.tile(shape, dtype, name=name, align_bytes=64)
+            return reuse.tile(shape, dtype, name=name, align_bytes=64, offset=offset)
+
+        def cleared_plane(width, name, offset=None):
+            plane = placed([P, width], U8, name, offset)
             nc.vector.memset(plane[:].bitcast(I32), 0)
             return plane
 
-        def load_plane(queue, plane, scales):
-            for q in range(4):
-                queue.dma_start(plane[32 * q : 32 * q + 4, :].bitcast(I32), scales[0, 4 * q : 4 * q + 4, :].bitcast(I32))
-
-        def load_staged_scales(queue, scales, name):
-            staged = keep.tile([4, 4, R // 4], I32, name=name)
+        def load_staged_scales(queue, scales, width, name):
+            staged = keep.tile([4, 4, width // 4], I32, name=name)
             queue.dma_start(staged[:], scales[0].bitcast(I32).rearrange("(q i) n -> i q n", i=4))
             return staged
 
@@ -57,79 +59,78 @@ def tile_picked_tokens_plain_twin_aboveaverage_store_plain_kernel(
             for q in range(4):
                 nc.vector.tensor_copy(plane[32 * q : 32 * q + 4, :].bitcast(I32), staged[:, q, :])
 
+        def load_plane(queue, plane, scales):
+            for q in range(4):
+                queue.dma_start(plane[32 * q : 32 * q + 4, :].bitcast(I32), scales[0, 4 * q : 4 * q + 4, :].bitcast(I32))
+
+        SLOT = 2048
+        xt_at = SLOT
+        w2_staged = load_staged_scales(nc.scalar, w2_scales, R, "w2_staged")
         xt_plane = cleared_plane(T, "xt_plane")
-        tok_list = load_list(offs, "tok_list")
-        w2_staged = load_staged_scales(nc.scalar, w2_scales, "w2_staged")
         load_plane(nc.scalar, xt_plane, xt_scales)
+        tok_list = load_list(offs, "tok_list")
+        b_list = load_list(offs3, "b_list")
         w2_raw = keep.tile([P, 2 * R], U8, name="w2_raw")
         nc.sync.dma_start(w2_raw[:].bitcast(I32), w2_words[0].bitcast(I32))
-        xt_raw = keep.tile([P, T], U32, name="xt_raw")
+        xt_raw = placed([P, T], U32, "xt_raw", xt_at)
         nc.sync.dma_start(xt_raw[:].bitcast(I32), xt_words[0].rearrange("p n t -> p (n t)").bitcast(I32))
-        b_list = load_list(offs3, "b_list")
-        w_staged = load_staged_scales(nc.sync, w_scales, "w_staged")
-        w_raw = keep.tile([P, R], I32, name="w_raw")
-        nc.sync.dma_start(w_raw[:], w_words[0].rearrange("p n t -> p (n t)").bitcast(I32))
         a_list = load_list(offs2, "a_list")
-        vs_list = load_list(offs5, "vs_list")
-        vs_raw = keep.tile([P, S], U16, name="vs_raw")
-        nc.sync.dma_start(vs_raw[:].bitcast(I32), vs_words[0].bitcast(I32))
         w2_plane = cleared_plane(R, "w2_plane")
-        w_plane = cleared_plane(R, "w_plane")
         boards_b = []
         boards_a = []
         for i in range(2):
             boards_b.append(keep.tile([P, C], F32, name=f"board_b{i}"))
             nc.vector.memset(boards_b[i][:], 0.0)
+        w_plane = cleared_plane(R, "w_plane")
+        for i in range(2):
             boards_a.append(keep.tile([P, C], F32, name=f"board_a{i}"))
             nc.vector.memset(boards_a[i][:], 0.0)
-        vs_plane = cleared_plane(S, "vs_plane")
-        load_plane(nc.sync, vs_plane, vs_scales)
+        w_raw = keep.tile([P, R], I32, name="w_raw")
+        nc.sync.dma_start(w_raw[:], w_words[0].rearrange("p n t -> p (n t)").bitcast(I32))
+        load_plane(nc.sync, w_plane, w_scales)
+        vs_list = load_list(offs5, "vs_list")
+        vs_raw = keep.tile([P, S], U16, name="vs_raw")
+        nc.sync.dma_start(vs_raw[:].bitcast(I32), vs_words[0].bitcast(I32))
         place_list = load_list(offs4, "place_list")
         sa_sb = keep.tile([P, PACK], F32, name="sa_sb")
         nc.sync.dma_start(sa_sb[:], sa.rearrange("(p t) one -> p (t one)", t=PACK))
 
-        def deal(raw, dtype, per_column, t0, t1, name):
-            dealt = keep.tile([P, t1 - t0, P * per_column], dtype, name=name, align_bytes=64)
+        def deal(raw, dtype, per_column, t, name, offset):
+            dealt = placed([P, P * per_column], dtype, name, offset)
             nc.vector.tensor_copy(
-                dealt[:].rearrange("p t (m b) -> p t m b", b=per_column),
-                raw[:].rearrange("p (m t b) -> p t m b", t=PACK, b=per_column)[:, t0:t1, :, :],
+                dealt[:].rearrange("p (m b) -> p m b", b=per_column),
+                raw[:].rearrange("p (m t b) -> p t m b", t=PACK, b=per_column)[:, t, :, :],
             )
-            return [dealt[:, t, :] for t in range(t1 - t0)]
+            return dealt[:]
+
+        def deal_b(t, slot):
+            plane = deal(w2_plane, U8, 1, t, f"w2_plane_{t}", slot * SLOT)
+            return deal(w2_raw, U8, 2, t, f"w2_words_{t}", slot * SLOT + P).bitcast(FP4X4), plane
+
+        def deal_a(t, slot):
+            plane = deal(w_plane, U8, 1, t, f"w_plane_{t}", slot * SLOT)
+            return deal(w_raw, I32, 1, t, f"w_words_{t}", slot * SLOT + P).bitcast(FP8X4), plane
 
         xg_words = keep.tile([P, J], U32, name="xg_words", align_bytes=64)
-        xg_plane = keep.tile([P, J], U8, name="xg_plane", align_bytes=64)
+        xg_planes = [placed([P, HALF], U8, "xg_plane0", None), placed([P, HALF], U8, "xg_plane1", 2 * SLOT)]
 
-        def product_to_board(words, plane, board, board_list, first, count, name, tag):
-            acc = psum.tile([P, count], F32, name="acc")
-            nc.tensor.matmul_mx(
-                out=acc[:], lhsT=words, lhsT_scale=plane,
-                rhs=xg_words[:, first : first + count].bitcast(FP8X4), rhs_scale=xg_plane[:, first : first + count],
-                start=True, stop=True,
-            )
-            result = keep.tile([P, count], F32, name=name, tag=tag, align_bytes=64)
-            nc.vector.tensor_copy(result[:], acc[:])
+        def product(dealt, halves, name, tag, on_scalar=False):
+            acc = psum.tile([P, len(halves), HALF], F32, name="acc")
+            for i, h in enumerate(halves):
+                nc.tensor.matmul_mx(
+                    out=acc[:, i, :], lhsT=dealt[0], lhsT_scale=dealt[1],
+                    rhs=xg_words[:, h * HALF : (h + 1) * HALF].bitcast(FP8X4), rhs_scale=xg_planes[h][:],
+                    start=True, stop=True,
+                )
+            result = keep.tile([P, len(halves) * HALF], F32, name=name, tag=tag, align_bytes=64)
+            if on_scalar:
+                nc.scalar.activation(result[:], acc[:].rearrange("p h j -> p (h j)"), COPY)
+            else:
+                nc.vector.tensor_copy(result[:], acc[:].rearrange("p h j -> p (h j)"))
+            return result
+
+        def put(board, board_list, first, count, result):
             nc.scalar.activation(board[:].indirect(entries(board_list, first, count)), result[:], COPY)
-
-        spread(w2_plane, w2_staged)
-        w2_plane_t = deal(w2_plane, U8, 1, 0, 1, "w2_plane_first")
-        w2_words_t = deal(w2_raw, U8, 2, 0, 1, "w2_words_first")
-        for first in range(0, J, HALF):
-            cols = slice(first, first + HALF)
-            nc.vector.tensor_copy(xg_plane[:, cols], xt_plane[:].indirect(entries(tok_list, first, HALF)))
-            nc.vector.tensor_copy(xg_words[:, cols], xt_raw[:].indirect(entries(tok_list, first, HALF)))
-            product_to_board(w2_words_t[0].bitcast(FP4X4), w2_plane_t[0], boards_b[0], b_list, first, HALF,
-                             f"b0_{first}", f"b0_{first}")
-        spread(w_plane, w_staged)
-        w_plane_t = deal(w_plane, U8, 1, 0, 1, "w_plane_first")
-        w_words_t = deal(w_raw, I32, 1, 0, 1, "w_words_first")
-        product_to_board(w_words_t[0].bitcast(FP8X4), w_plane_t[0], boards_a[0], a_list, 0, J, "a0", "a0")
-        w2_plane_t = w2_plane_t + deal(w2_plane, U8, 1, 1, PACK, "w2_plane_rest")
-        w2_words_t = w2_words_t + deal(w2_raw, U8, 2, 1, PACK, "w2_words_rest")
-        w_plane_t = w_plane_t + deal(w_plane, U8, 1, 1, PACK, "w_plane_rest")
-        w_words_t = w_words_t + deal(w_raw, I32, 1, 1, PACK, "w_words_rest")
-
-        vg_words = keep.tile([P, N], U16, name="vg_words", align_bytes=64)
-        vg_plane = keep.tile([P, N], U8, name="vg_plane", align_bytes=64)
 
         g1 = []
 
@@ -146,15 +147,34 @@ def tile_picked_tokens_plain_twin_aboveaverage_store_plain_kernel(
             nc.vector.tensor_scalar(out=g[:], in0=pg[:], scalar1=mean[:], scalar2=0.0, op0=ALU.subtract, op1=ALU.max)
             g1.append(g)
 
-        for t in range(1, PACK):
-            product_to_board(w2_words_t[t].bitcast(FP4X4), w2_plane_t[t], boards_b[t % 2], b_list, 0, J, f"b{t}", f"b{t}")
-            product_to_board(w_words_t[t].bitcast(FP8X4), w_plane_t[t], boards_a[t % 2], a_list, 0, J, f"a{t}",
-                             "last" if t == PACK - 1 else f"a{t}")
-            if t == 1:
-                nc.vector.tensor_copy(vg_words[:], vs_raw[:].indirect(vs_list[:]))
-                nc.vector.tensor_copy(vg_plane[:], vs_plane[:].indirect(vs_list[:]))
-            above_average(t - 1)
-        above_average(PACK - 1)
+        spread(w2_plane, w2_staged)
+        dealt = deal_b(0, 0)
+        nc.vector.tensor_copy(xg_planes[0][:], xt_plane[:].indirect(entries(tok_list, 0, HALF)))
+        for h in range(2):
+            nc.vector.tensor_copy(xg_words[:, h * HALF : (h + 1) * HALF], xt_raw[:].indirect(entries(tok_list, h * HALF, HALF)))
+        nc.vector.tensor_copy(xg_planes[1][:], xt_plane[:].indirect(entries(tok_list, HALF, HALF)))
+        for h in range(2):
+            put(boards_b[0], b_list, h * HALF, HALF, product(dealt, [h], f"b0_{h}", ("first", "b0_1")[h], on_scalar=h == 0))
+        put(boards_b[1], b_list, 0, J, product(deal_b(1, 1), [0, 1], "b1", "first"))
+        for t in range(2):
+            put(boards_a[t], a_list, 0, J, product(deal_a(t, t), [0, 1], f"a{t}", f"a{t}"))
+        vs_plane = cleared_plane(S, "vs_plane", 2 * SLOT + 1024)
+        load_plane(nc.sync, vs_plane, vs_scales)
+        for t in range(2, PACK):
+            b_result = product(deal_b(t, 0), [0, 1], f"b{t}", f"b{t}")
+            a_result = product(deal_a(t, 1), [0, 1], f"a{t}", "last" if t == PACK - 1 else f"a{t}")
+            if t == 2:
+                above_average(0)
+            put(boards_b[t % 2], b_list, 0, J, b_result)
+            put(boards_a[t % 2], a_list, 0, J, a_result)
+            if t == 2:
+                above_average(1)
+        vg_plane = placed([P, N], U8, "vg_plane", SLOT)
+        vg_words = placed([P, N], U16, "vg_words", SLOT + N)
+        nc.vector.tensor_copy(vg_words[:], vs_raw[:].indirect(vs_list[:]))
+        nc.vector.tensor_copy(vg_plane[:], vs_plane[:].indirect(vs_list[:]))
+        above_average(2)
+        above_average(3)
 
         hid = keep.tile([P, PACK, O], BF16, name="hid", tag="last", align_bytes=64)
         for t in range(PACK - 1):

@@ -63,8 +63,8 @@ def tile_picked_tokens_plain_twin_aboveaverage_store_plain_kernel(
             for q in range(4):
                 queue.dma_start(plane[32 * q : 32 * q + 4, :].bitcast(I32), scales[0, 4 * q : 4 * q + 4, :].bitcast(I32))
 
-        SLOT = 2048
-        xt_at = SLOT
+        SLOTS = (192, 2560)
+        xt_at = SLOTS[1]
         w2_staged = load_staged_scales(nc.scalar, w2_scales, R, "w2_staged")
         xt_plane = cleared_plane(T, "xt_plane")
         load_plane(nc.scalar, xt_plane, xt_scales)
@@ -104,15 +104,16 @@ def tile_picked_tokens_plain_twin_aboveaverage_store_plain_kernel(
             return dealt[:]
 
         def deal_b(t, slot):
-            plane = deal(w2_plane, U8, 1, t, f"w2_plane_{t}", slot * SLOT)
-            return deal(w2_raw, U8, 2, t, f"w2_words_{t}", slot * SLOT + P).bitcast(FP4X4), plane
+            plane_at, words_at = (256, 0) if t == 3 else (SLOTS[slot], SLOTS[slot] + P)
+            plane = deal(w2_plane, U8, 1, t, f"w2_plane_{t}", plane_at)
+            return deal(w2_raw, U8, 2, t, f"w2_words_{t}", words_at).bitcast(FP4X4), plane
 
         def deal_a(t, slot):
-            plane = deal(w_plane, U8, 1, t, f"w_plane_{t}", slot * SLOT)
-            return deal(w_raw, I32, 1, t, f"w_words_{t}", slot * SLOT + P).bitcast(FP8X4), plane
+            plane = deal(w_plane, U8, 1, t, f"w_plane_{t}", SLOTS[slot])
+            return deal(w_raw, I32, 1, t, f"w_words_{t}", SLOTS[slot] + P).bitcast(FP8X4), plane
 
         xg_words = keep.tile([P, J], U32, name="xg_words", align_bytes=64)
-        xg_planes = [placed([P, HALF], U8, "xg_plane0", None), placed([P, HALF], U8, "xg_plane1", 2 * SLOT)]
+        xg_planes = [placed([P, HALF], U8, "xg_plane0", None), placed([P, HALF], U8, "xg_plane1", xt_at + 2048)]
 
         def product(dealt, halves, name, tag, on_scalar=False):
             acc = psum.tile([P, len(halves), HALF], F32, name="acc")
@@ -135,7 +136,7 @@ def tile_picked_tokens_plain_twin_aboveaverage_store_plain_kernel(
         g1 = []
 
         def above_average(t):
-            pg = keep.tile([P, C], F32, name=f"pg{t}")
+            pg = placed([P, C], F32, f"pg{t}", (512, 576, 576, None)[t])
             total = keep.tile([P, 1], F32, name=f"total{t}")
             nc.vector.scalar_tensor_tensor(
                 out=pg[:], in0=boards_a[t % 2][:], scalar=1.0, in1=boards_b[t % 2][:],
@@ -158,19 +159,16 @@ def tile_picked_tokens_plain_twin_aboveaverage_store_plain_kernel(
         put(boards_b[1], b_list, 0, J, product(deal_b(1, 1), [0, 1], "b1", "first"))
         for t in range(2):
             put(boards_a[t], a_list, 0, J, product(deal_a(t, t), [0, 1], f"a{t}", f"a{t}"))
-        vs_plane = cleared_plane(S, "vs_plane", 2 * SLOT + 1024)
+        vs_plane = cleared_plane(S, "vs_plane", xt_at + 3072)
         load_plane(nc.sync, vs_plane, vs_scales)
         for t in range(2, PACK):
             b_result = product(deal_b(t, 0), [0, 1], f"b{t}", f"b{t}")
             a_result = product(deal_a(t, 1), [0, 1], f"a{t}", "last" if t == PACK - 1 else f"a{t}")
-            if t == 2:
-                above_average(0)
+            above_average(t - 2)
             put(boards_b[t % 2], b_list, 0, J, b_result)
             put(boards_a[t % 2], a_list, 0, J, a_result)
-            if t == 2:
-                above_average(1)
-        vg_plane = placed([P, N], U8, "vg_plane", SLOT)
-        vg_words = placed([P, N], U16, "vg_words", SLOT + N)
+        vg_plane = placed([P, N], U8, "vg_plane", SLOTS[1] + 64)
+        vg_words = placed([P, N], U16, "vg_words", SLOTS[1] + 64 + N)
         nc.vector.tensor_copy(vg_words[:], vs_raw[:].indirect(vs_list[:]))
         nc.vector.tensor_copy(vg_plane[:], vs_plane[:].indirect(vs_list[:]))
         above_average(2)

@@ -20,6 +20,21 @@ P = 128
 PACK = 4
 HALF = 128
 LIST_ROWS = 16
+QUADRANTS = 4
+SCALE_ROWS = 4
+BOARDS = 2
+ALIGN = 64
+
+SLOTS = (3 * ALIGN, 3 * ALIGN + P + 2 * P - ALIGN + 4 * C)
+XT_WORDS_AT = SLOTS[1]
+XG_PLANE1_AT = XT_WORDS_AT + 2 * T
+VS_PLANE_AT = XT_WORDS_AT + 3 * T
+B3_WORDS_AT = SLOTS[0] + ALIGN - 2 * P
+B3_PLANE_AT = SLOTS[0] + ALIGN
+PG_FIRST_AT = SLOTS[1] - 4 * C
+PG_REST_AT = SLOTS[1] + ALIGN - 4 * C
+VG_PLANE_AT = SLOTS[1] + ALIGN
+VG_WORDS_AT = VG_PLANE_AT + N
 
 
 def tile_picked_tokens_plain_twin_aboveaverage_store_plain_kernel(
@@ -41,50 +56,41 @@ def tile_picked_tokens_plain_twin_aboveaverage_store_plain_kernel(
             return tile[:, first // LIST_ROWS : (first + count) // LIST_ROWS]
 
         def placed(shape, dtype, name, offset):
-            if offset is None:
-                return keep.tile(shape, dtype, name=name, align_bytes=64)
-            return reuse.tile(shape, dtype, name=name, align_bytes=64, offset=offset)
+            return reuse.tile(shape, dtype, name=name, align_bytes=ALIGN, offset=offset)
 
-        def cleared_plane(width, name, offset=None):
-            plane = placed([P, width], U8, name, offset)
+        def clear(plane):
             nc.vector.memset(plane[:].bitcast(I32), 0)
-            return plane
 
-        def load_staged_scales(queue, scales, width, name):
-            staged = keep.tile([4, 4, width // 4], I32, name=name)
-            queue.dma_start(staged[:], scales[0].bitcast(I32).rearrange("(q i) n -> i q n", i=4))
-            return staged
-
-        def spread(plane, staged):
-            for q in range(4):
-                nc.vector.tensor_copy(plane[32 * q : 32 * q + 4, :].bitcast(I32), staged[:, q, :])
+        def quadrant_rows(plane, q):
+            return plane[32 * q : 32 * q + SCALE_ROWS, :].bitcast(I32)
 
         def load_plane(queue, plane, scales):
-            for q in range(4):
-                queue.dma_start(plane[32 * q : 32 * q + 4, :].bitcast(I32), scales[0, 4 * q : 4 * q + 4, :].bitcast(I32))
+            for q in range(QUADRANTS):
+                queue.dma_start(quadrant_rows(plane, q), scales[0, SCALE_ROWS * q : SCALE_ROWS * (q + 1), :].bitcast(I32))
 
-        SLOTS = (192, 2560)
-        xt_at = SLOTS[1]
-        w2_staged = load_staged_scales(nc.scalar, w2_scales, R, "w2_staged")
-        xt_plane = cleared_plane(T, "xt_plane")
+        def cleared_board(name):
+            board = keep.tile([P, C], F32, name=name)
+            nc.vector.memset(board[:], 0.0)
+            return board
+
+        w2_staged = keep.tile([SCALE_ROWS, QUADRANTS, R // 4], I32, name="w2_staged")
+        nc.scalar.dma_start(w2_staged[:], w2_scales[0].bitcast(I32).rearrange("(q i) n -> i q n", i=SCALE_ROWS))
+        xt_plane = keep.tile([P, T], U8, name="xt_plane", align_bytes=ALIGN)
+        clear(xt_plane)
         load_plane(nc.scalar, xt_plane, xt_scales)
         tok_list = load_list(offs, "tok_list")
         b_list = load_list(offs3, "b_list")
         w2_raw = keep.tile([P, 2 * R], U8, name="w2_raw")
         nc.sync.dma_start(w2_raw[:].bitcast(I32), w2_words[0].bitcast(I32))
-        xt_raw = placed([P, T], U32, "xt_raw", xt_at)
+        xt_raw = placed([P, T], U32, "xt_raw", XT_WORDS_AT)
         nc.sync.dma_start(xt_raw[:].bitcast(I32), xt_words[0].rearrange("p n t -> p (n t)").bitcast(I32))
         a_list = load_list(offs2, "a_list")
-        w2_plane = cleared_plane(R, "w2_plane")
-        boards_b = []
-        boards_a = []
-        for i in range(2):
-            boards_b.append(keep.tile([P, C], F32, name=f"board_b{i}"))
-            nc.vector.memset(boards_b[i][:], 0.0)
-        w_plane = cleared_plane(R, "w_plane")
-        for i in range(2):
-            boards_a.append(keep.tile([P, C], F32, name=f"board_a{i}"))
-            nc.vector.memset(boards_a[i][:], 0.0)
+        w2_plane = keep.tile([P, R], U8, name="w2_plane", align_bytes=ALIGN)
+        clear(w2_plane)
+        boards_b = [cleared_board(f"board_b{i}") for i in range(BOARDS)]
+        w_plane = keep.tile([P, R], U8, name="w_plane", align_bytes=ALIGN)
+        clear(w_plane)
+        boards_a = [cleared_board(f"board_a{i}") for i in range(BOARDS)]
         w_raw = keep.tile([P, R], I32, name="w_raw")
         nc.sync.dma_start(w_raw[:], w_words[0].rearrange("p n t -> p (n t)").bitcast(I32))
         load_plane(nc.sync, w_plane, w_scales)
@@ -103,8 +109,7 @@ def tile_picked_tokens_plain_twin_aboveaverage_store_plain_kernel(
             )
             return dealt[:]
 
-        def deal_b(t, slot):
-            plane_at, words_at = (256, 0) if t == 3 else (SLOTS[slot], SLOTS[slot] + P)
+        def deal_b(t, plane_at, words_at):
             plane = deal(w2_plane, U8, 1, t, f"w2_plane_{t}", plane_at)
             return deal(w2_raw, U8, 2, t, f"w2_words_{t}", words_at).bitcast(FP4X4), plane
 
@@ -112,97 +117,111 @@ def tile_picked_tokens_plain_twin_aboveaverage_store_plain_kernel(
             plane = deal(w_plane, U8, 1, t, f"w_plane_{t}", SLOTS[slot])
             return deal(w_raw, I32, 1, t, f"w_words_{t}", SLOTS[slot] + P).bitcast(FP8X4), plane
 
-        xg_words = keep.tile([P, J], U32, name="xg_words", align_bytes=64)
-        xg_planes = [placed([P, HALF], U8, "xg_plane0", None), placed([P, HALF], U8, "xg_plane1", xt_at + 2048)]
+        xg_words = keep.tile([P, J], U32, name="xg_words", align_bytes=ALIGN)
+        xg_planes = [
+            keep.tile([P, HALF], U8, name="xg_plane0", align_bytes=ALIGN),
+            placed([P, HALF], U8, "xg_plane1", XG_PLANE1_AT),
+        ]
 
-        def product(dealt, halves, name, tag, on_scalar=False):
+        def multiply(dealt, halves):
+            words, plane = dealt
             acc = psum.tile([P, len(halves), HALF], F32, name="acc")
             for i, h in enumerate(halves):
                 nc.tensor.matmul_mx(
-                    out=acc[:, i, :], lhsT=dealt[0], lhsT_scale=dealt[1],
+                    out=acc[:, i, :], lhsT=words, lhsT_scale=plane,
                     rhs=xg_words[:, h * HALF : (h + 1) * HALF].bitcast(FP8X4), rhs_scale=xg_planes[h][:],
                     start=True, stop=True,
                 )
-            result = keep.tile([P, len(halves) * HALF], F32, name=name, tag=tag, align_bytes=64)
-            if on_scalar:
-                nc.scalar.activation(result[:], acc[:].rearrange("p h j -> p (h j)"), COPY)
-            else:
-                nc.vector.tensor_copy(result[:], acc[:].rearrange("p h j -> p (h j)"))
+            return acc[:].rearrange("p h j -> p (h j)")
+
+        def product(dealt, halves, name, tag):
+            sums = multiply(dealt, halves)
+            result = keep.tile([P, len(halves) * HALF], F32, name=name, tag=tag, align_bytes=ALIGN)
+            nc.vector.tensor_copy(result[:], sums)
             return result
 
         def put(board, board_list, first, count, result):
             nc.scalar.activation(board[:].indirect(entries(board_list, first, count)), result[:], COPY)
 
-        g1 = []
-
         def above_average(t):
-            pg = placed([P, C], F32, f"pg{t}", (512, 576, 576, None)[t])
+            pg = placed([P, C], F32, f"pg{t}", PG_FIRST_AT if t == 0 else PG_REST_AT)
             total = keep.tile([P, 1], F32, name=f"total{t}")
             nc.vector.scalar_tensor_tensor(
-                out=pg[:], in0=boards_a[t % 2][:], scalar=1.0, in1=boards_b[t % 2][:],
+                out=pg[:], in0=boards_a[t % BOARDS][:], scalar=1.0, in1=boards_b[t % BOARDS][:],
                 op0=ALU.mult, op1=ALU.max, accum_out=total[:],
             )
             mean = keep.tile([P, 1], F32, name=f"mean{t}")
             nc.vector.tensor_scalar(out=mean[:], in0=total[:], scalar1=1.0 / C, scalar2=None, op0=ALU.mult)
-            g = keep.tile([P, C], F32, name=f"g1_{t}")
-            nc.vector.tensor_scalar(out=g[:], in0=pg[:], scalar1=mean[:], scalar2=0.0, op0=ALU.subtract, op1=ALU.max)
-            g1.append(g)
+            above = keep.tile([P, C], F32, name=f"g1_{t}")
+            nc.vector.tensor_scalar(out=above[:], in0=pg[:], scalar1=mean[:], scalar2=0.0, op0=ALU.subtract, op1=ALU.max)
+            return above
 
-        spread(w2_plane, w2_staged)
-        dealt = deal_b(0, 0)
+        for q in range(QUADRANTS):
+            nc.vector.tensor_copy(quadrant_rows(w2_plane, q), w2_staged[:, q, :])
+        dealt_b0 = deal_b(0, SLOTS[0], SLOTS[0] + P)
         nc.vector.tensor_copy(xg_planes[0][:], xt_plane[:].indirect(entries(tok_list, 0, HALF)))
         for h in range(2):
             nc.vector.tensor_copy(xg_words[:, h * HALF : (h + 1) * HALF], xt_raw[:].indirect(entries(tok_list, h * HALF, HALF)))
         nc.vector.tensor_copy(xg_planes[1][:], xt_plane[:].indirect(entries(tok_list, HALF, HALF)))
-        for h in range(2):
-            put(boards_b[0], b_list, h * HALF, HALF, product(dealt, [h], f"b0_{h}", ("first", "b0_1")[h], on_scalar=h == 0))
-        put(boards_b[1], b_list, 0, J, product(deal_b(1, 1), [0, 1], "b1", "first"))
-        for t in range(2):
+        first_sums = multiply(dealt_b0, [0])
+        first_piece = keep.tile([P, HALF], F32, name="b0_0", tag="first", align_bytes=ALIGN)
+        nc.scalar.activation(first_piece[:], first_sums, COPY)
+        put(boards_b[0], b_list, 0, HALF, first_piece)
+        put(boards_b[0], b_list, HALF, HALF, product(dealt_b0, [1], "b0_1", "b0_1"))
+        put(boards_b[1], b_list, 0, J, product(deal_b(1, SLOTS[1], SLOTS[1] + P), [0, 1], "b1", "first"))
+        for t in range(BOARDS):
             put(boards_a[t], a_list, 0, J, product(deal_a(t, t), [0, 1], f"a{t}", f"a{t}"))
-        vs_plane = cleared_plane(S, "vs_plane", xt_at + 3072)
+        vs_plane = placed([P, S], U8, "vs_plane", VS_PLANE_AT)
+        clear(vs_plane)
         load_plane(nc.sync, vs_plane, vs_scales)
-        for t in range(2, PACK):
-            b_result = product(deal_b(t, 0), [0, 1], f"b{t}", f"b{t}")
+
+        g1 = []
+        b_places = {2: (SLOTS[0], SLOTS[0] + P), 3: (B3_PLANE_AT, B3_WORDS_AT)}
+        for t in range(BOARDS, PACK):
+            b_result = product(deal_b(t, *b_places[t]), [0, 1], f"b{t}", f"b{t}")
             a_result = product(deal_a(t, 1), [0, 1], f"a{t}", "last" if t == PACK - 1 else f"a{t}")
-            above_average(t - 2)
-            put(boards_b[t % 2], b_list, 0, J, b_result)
-            put(boards_a[t % 2], a_list, 0, J, a_result)
-        vg_plane = placed([P, N], U8, "vg_plane", SLOTS[1] + 64)
-        vg_words = placed([P, N], U16, "vg_words", SLOTS[1] + 64 + N)
+            g1.append(above_average(t - BOARDS))
+            put(boards_b[t % BOARDS], b_list, 0, J, b_result)
+            put(boards_a[t % BOARDS], a_list, 0, J, a_result)
+
+        vg_plane = placed([P, N], U8, "vg_plane", VG_PLANE_AT)
+        vg_words = placed([P, N], U16, "vg_words", VG_WORDS_AT)
         nc.vector.tensor_copy(vg_words[:], vs_raw[:].indirect(vs_list[:]))
         nc.vector.tensor_copy(vg_plane[:], vs_plane[:].indirect(vs_list[:]))
-        above_average(2)
-        above_average(3)
+        for t in range(BOARDS, PACK):
+            g1.append(above_average(t))
 
-        hid = keep.tile([P, PACK, O], BF16, name="hid", tag="last", align_bytes=64)
+        hid = keep.tile([P, PACK, O], BF16, name="hid", tag="last", align_bytes=ALIGN)
         for t in range(PACK - 1):
             nc.scalar.activation(hid[:, t, :], g1[t][:].indirect(place_list[:]), COPY, scale=sa_sb[:, t : t + 1])
-        t = PACK - 1
         for first in range(0, O, HALF):
-            nc.scalar.activation(hid[:, t, first : first + HALF], g1[t][:].indirect(entries(place_list, first, HALF)),
-                                 COPY, scale=sa_sb[:, t : t + 1])
+            nc.scalar.activation(hid[:, PACK - 1, first : first + HALF],
+                                 g1[PACK - 1][:].indirect(entries(place_list, first, HALF)),
+                                 COPY, scale=sa_sb[:, PACK - 1 : PACK])
+
         grouped = []
         for first in range(0, O, HALF):
-            tile = keep.tile([P, HALF, PACK], BF16, name=f"grouped{first}", align_bytes=64)
+            tile = keep.tile([P, HALF, PACK], BF16, name=f"grouped{first}", align_bytes=ALIGN)
             nc.vector.tensor_copy(tile[:], hid[:, :, first : first + HALF].rearrange("p t o -> p o t"))
             grouped.append(tile)
+
         out_view = out.rearrange("(b p) o -> p b o", p=P)
         for h in range(2):
-            codes = keep.tile([P, HALF], U32, name=f"hid_words{h}", align_bytes=64)
-            plane = keep.tile([P, HALF], U8, name=f"hid_plane{h}", align_bytes=64)
-            nc.vector.quantize_mx(out=codes[:].bitcast(FP8X4), scales=plane[:],
+            codes = keep.tile([P, HALF], U32, name=f"hid_words{h}", align_bytes=ALIGN)
+            scales = keep.tile([P, HALF], U8, name=f"hid_plane{h}", align_bytes=ALIGN)
+            nc.vector.quantize_mx(out=codes[:].bitcast(FP8X4), scales=scales[:],
                                   in_=grouped[h][:].rearrange("p o t -> p (o t)"))
-            cols = slice(h * HALF, (h + 1) * HALF)
-            for b in range(2):
+            for block in range(N // P):
+                rows = slice(block * P, (block + 1) * P)
                 y = psum.tile([P, HALF], F32, name="y")
                 nc.tensor.matmul_mx(
-                    out=y[:], lhsT=vg_words[:, b * P : (b + 1) * P].bitcast(FP4X4), lhsT_scale=vg_plane[:, b * P : (b + 1) * P],
-                    rhs=codes[:].bitcast(FP8X4), rhs_scale=plane[:], start=True, stop=True,
+                    out=y[:], lhsT=vg_words[:, rows].bitcast(FP4X4), lhsT_scale=vg_plane[:, rows],
+                    rhs=codes[:].bitcast(FP8X4), rhs_scale=scales[:], start=True, stop=True,
                 )
-                y_sb = keep.tile([P, HALF], F32, name=f"y{h}{b}")
-                if h == 1 and b == 0:
+                y_sb = keep.tile([P, HALF], F32, name=f"y{h}{block}")
+                if (h, block) == (1, 0):
                     nc.vector.tensor_copy(y_sb[:], y[:])
                 else:
                     nc.scalar.copy(y_sb[:], y[:])
-                queue = nc.scalar if h == 1 and b == 1 else nc.sync
-                queue.dma_start(out_view[:, b, cols], y_sb[:])
+                queue = nc.scalar if (h, block) == (1, 1) else nc.sync
+                queue.dma_start(out_view[:, block, h * HALF : (h + 1) * HALF], y_sb[:])

from contextlib import ExitStack

import concourse.mybir as mybir

K, J, R, T, C, O, N, S = 512, 256, 512, 1024, 512, 256, 256, 1024
FLOPS = 2 * K * R * J * 2 + 2 * R * N * O

F32 = mybir.dt.float32
BF16 = mybir.dt.bfloat16
I32 = mybir.dt.int32
U32 = mybir.dt.uint32
U16 = mybir.dt.uint16
U8 = mybir.dt.uint8
FP8X4 = mybir.dt.float8_e4m3fn_x4
FP4X4 = mybir.dt.float4_e2m1fn_x4
ALU = mybir.AluOpType
COPY = mybir.ActivationFunctionType.Copy

P = 128
PACK = 4
HALF = 128
LIST_ROWS = 16
QUADRANTS = 4
SCALE_ROWS = 4
BOARDS = 2
ALIGN = 64

SLOTS = (3 * ALIGN, 3 * ALIGN + P + 2 * P - ALIGN + 4 * C)
XT_WORDS_AT = SLOTS[1]
XG_PLANE1_AT = XT_WORDS_AT + 2 * T
VS_PLANE_AT = XT_WORDS_AT + 3 * T
B3_WORDS_AT = SLOTS[0] + ALIGN - 2 * P
B3_PLANE_AT = SLOTS[0] + ALIGN
PG_FIRST_AT = SLOTS[1] - 4 * C
PG_REST_AT = SLOTS[1] + ALIGN - 4 * C
VG_PLANE_AT = SLOTS[1] + ALIGN
VG_WORDS_AT = VG_PLANE_AT + N


def tile_picked_tokens_plain_twin_aboveaverage_store_plain_kernel(
    tc, xt_words, xt_scales, w_words, w_scales, w2_words, w2_scales, sa, vs_words, vs_scales,
    offs, offs2, offs3, offs4, offs5, out,
):
    nc = tc.nc
    with ExitStack() as ctx:
        keep = ctx.enter_context(tc.tile_pool(name="keep", bufs=1))
        reuse = ctx.enter_context(tc.tile_pool(name="reuse", bufs=1))
        psum = ctx.enter_context(tc.psum_pool(name="psum", bufs=4))

        def load_list(dram, name):
            tile = keep.tile([P, J // LIST_ROWS], U16, name=name)
            nc.sync.dma_start(tile[:], dram)
            return tile

        def entries(tile, first, count):
            return tile[:, first // LIST_ROWS : (first + count) // LIST_ROWS]

        def placed(shape, dtype, name, offset):
            return reuse.tile(shape, dtype, name=name, align_bytes=ALIGN, offset=offset)

        def clear(plane):
            nc.vector.memset(plane[:].bitcast(I32), 0)

        def quadrant_rows(plane, q):
            return plane[32 * q : 32 * q + SCALE_ROWS, :].bitcast(I32)

        def load_plane(queue, plane, scales):
            for q in range(QUADRANTS):
                queue.dma_start(quadrant_rows(plane, q), scales[0, SCALE_ROWS * q : SCALE_ROWS * (q + 1), :].bitcast(I32))

        def cleared_board(name):
            board = keep.tile([P, C], F32, name=name)
            nc.vector.memset(board[:], 0.0)
            return board

        w2_staged = keep.tile([SCALE_ROWS, QUADRANTS, R // 4], I32, name="w2_staged")
        nc.scalar.dma_start(w2_staged[:], w2_scales[0].bitcast(I32).rearrange("(q i) n -> i q n", i=SCALE_ROWS))
        xt_plane = keep.tile([P, T], U8, name="xt_plane", align_bytes=ALIGN)
        clear(xt_plane)
        load_plane(nc.scalar, xt_plane, xt_scales)
        tok_list = load_list(offs, "tok_list")
        b_list = load_list(offs3, "b_list")
        w2_raw = keep.tile([P, 2 * R], U8, name="w2_raw")
        nc.sync.dma_start(w2_raw[:].bitcast(I32), w2_words[0].bitcast(I32))
        xt_raw = placed([P, T], U32, "xt_raw", XT_WORDS_AT)
        nc.sync.dma_start(xt_raw[:].bitcast(I32), xt_words[0].rearrange("p n t -> p (n t)").bitcast(I32))
        a_list = load_list(offs2, "a_list")
        w2_plane = keep.tile([P, R], U8, name="w2_plane", align_bytes=ALIGN)
        clear(w2_plane)
        boards_b = [cleared_board(f"board_b{i}") for i in range(BOARDS)]
        w_plane = keep.tile([P, R], U8, name="w_plane", align_bytes=ALIGN)
        clear(w_plane)
        boards_a = [cleared_board(f"board_a{i}") for i in range(BOARDS)]
        w_raw = keep.tile([P, R], I32, name="w_raw")
        nc.sync.dma_start(w_raw[:], w_words[0].rearrange("p n t -> p (n t)").bitcast(I32))
        load_plane(nc.sync, w_plane, w_scales)
        vs_list = load_list(offs5, "vs_list")
        vs_raw = keep.tile([P, S], U16, name="vs_raw")
        nc.sync.dma_start(vs_raw[:].bitcast(I32), vs_words[0].bitcast(I32))
        place_list = load_list(offs4, "place_list")
        sa_sb = keep.tile([P, PACK], F32, name="sa_sb")
        nc.sync.dma_start(sa_sb[:], sa.rearrange("(p t) one -> p (t one)", t=PACK))

        def deal(raw, dtype, per_column, t, name, offset):
            dealt = placed([P, P * per_column], dtype, name, offset)
            nc.vector.tensor_copy(
                dealt[:].rearrange("p (m b) -> p m b", b=per_column),
                raw[:].rearrange("p (m t b) -> p t m b", t=PACK, b=per_column)[:, t, :, :],
            )
            return dealt[:]

        def deal_b(t, plane_at, words_at):
            plane = deal(w2_plane, U8, 1, t, f"w2_plane_{t}", plane_at)
            return deal(w2_raw, U8, 2, t, f"w2_words_{t}", words_at).bitcast(FP4X4), plane

        def deal_a(t, slot):
            plane = deal(w_plane, U8, 1, t, f"w_plane_{t}", SLOTS[slot])
            return deal(w_raw, I32, 1, t, f"w_words_{t}", SLOTS[slot] + P).bitcast(FP8X4), plane

        xg_words = keep.tile([P, J], U32, name="xg_words", align_bytes=ALIGN)
        xg_planes = [
            keep.tile([P, HALF], U8, name="xg_plane0", align_bytes=ALIGN),
            placed([P, HALF], U8, "xg_plane1", XG_PLANE1_AT),
        ]

        def multiply(dealt, halves):
            words, plane = dealt
            acc = psum.tile([P, len(halves), HALF], F32, name="acc")
            for i, h in enumerate(halves):
                nc.tensor.matmul_mx(
                    out=acc[:, i, :], lhsT=words, lhsT_scale=plane,
                    rhs=xg_words[:, h * HALF : (h + 1) * HALF].bitcast(FP8X4), rhs_scale=xg_planes[h][:],
                    start=True, stop=True,
                )
            return acc[:].rearrange("p h j -> p (h j)")

        def product(dealt, halves, name, tag):
            sums = multiply(dealt, halves)
            result = keep.tile([P, len(halves) * HALF], F32, name=name, tag=tag, align_bytes=ALIGN)
            nc.vector.tensor_copy(result[:], sums)
            return result

        def put(board, board_list, first, count, result):
            nc.scalar.activation(board[:].indirect(entries(board_list, first, count)), result[:], COPY)

        def above_average(t):
            pg = placed([P, C], F32, f"pg{t}", PG_FIRST_AT if t == 0 else PG_REST_AT)
            total = keep.tile([P, 1], F32, name=f"total{t}")
            nc.vector.scalar_tensor_tensor(
                out=pg[:], in0=boards_a[t % BOARDS][:], scalar=1.0, in1=boards_b[t % BOARDS][:],
                op0=ALU.mult, op1=ALU.max, accum_out=total[:],
            )
            mean = keep.tile([P, 1], F32, name=f"mean{t}")
            nc.vector.tensor_scalar(out=mean[:], in0=total[:], scalar1=1.0 / C, scalar2=None, op0=ALU.mult)
            above = keep.tile([P, C], F32, name=f"g1_{t}")
            nc.vector.tensor_scalar(out=above[:], in0=pg[:], scalar1=mean[:], scalar2=0.0, op0=ALU.subtract, op1=ALU.max)
            return above

        for q in range(QUADRANTS):
            nc.vector.tensor_copy(quadrant_rows(w2_plane, q), w2_staged[:, q, :])
        dealt_b0 = deal_b(0, SLOTS[0], SLOTS[0] + P)
        nc.vector.tensor_copy(xg_planes[0][:], xt_plane[:].indirect(entries(tok_list, 0, HALF)))
        for h in range(2):
            nc.vector.tensor_copy(xg_words[:, h * HALF : (h + 1) * HALF], xt_raw[:].indirect(entries(tok_list, h * HALF, HALF)))
        nc.vector.tensor_copy(xg_planes[1][:], xt_plane[:].indirect(entries(tok_list, HALF, HALF)))
        first_sums = multiply(dealt_b0, [0])
        first_piece = keep.tile([P, HALF], F32, name="b0_0", tag="first", align_bytes=ALIGN)
        nc.scalar.activation(first_piece[:], first_sums, COPY)
        put(boards_b[0], b_list, 0, HALF, first_piece)
        put(boards_b[0], b_list, HALF, HALF, product(dealt_b0, [1], "b0_1", "b0_1"))
        put(boards_b[1], b_list, 0, J, product(deal_b(1, SLOTS[1], SLOTS[1] + P), [0, 1], "b1", "first"))
        for t in range(BOARDS):
            put(boards_a[t], a_list, 0, J, product(deal_a(t, t), [0, 1], f"a{t}", f"a{t}"))
        vs_plane = placed([P, S], U8, "vs_plane", VS_PLANE_AT)
        clear(vs_plane)
        load_plane(nc.sync, vs_plane, vs_scales)

        g1 = []
        b_places = {2: (SLOTS[0], SLOTS[0] + P), 3: (B3_PLANE_AT, B3_WORDS_AT)}
        for t in range(BOARDS, PACK):
            b_result = product(deal_b(t, *b_places[t]), [0, 1], f"b{t}", f"b{t}")
            a_result = product(deal_a(t, 1), [0, 1], f"a{t}", "last" if t == PACK - 1 else f"a{t}")
            g1.append(above_average(t - BOARDS))
            put(boards_b[t % BOARDS], b_list, 0, J, b_result)
            put(boards_a[t % BOARDS], a_list, 0, J, a_result)

        vg_plane = placed([P, N], U8, "vg_plane", VG_PLANE_AT)
        vg_words = placed([P, N], U16, "vg_words", VG_WORDS_AT)
        nc.vector.tensor_copy(vg_words[:], vs_raw[:].indirect(vs_list[:]))
        nc.vector.tensor_copy(vg_plane[:], vs_plane[:].indirect(vs_list[:]))
        for t in range(BOARDS, PACK):
            g1.append(above_average(t))

        hid = keep.tile([P, PACK, O], BF16, name="hid", tag="last", align_bytes=ALIGN)
        for t in range(PACK - 1):
            nc.scalar.activation(hid[:, t, :], g1[t][:].indirect(place_list[:]), COPY, scale=sa_sb[:, t : t + 1])
        for first in range(0, O, HALF):
            nc.scalar.activation(hid[:, PACK - 1, first : first + HALF],
                                 g1[PACK - 1][:].indirect(entries(place_list, first, HALF)),
                                 COPY, scale=sa_sb[:, PACK - 1 : PACK])

        grouped = []
        for first in range(0, O, HALF):
            tile = keep.tile([P, HALF, PACK], BF16, name=f"grouped{first}", align_bytes=ALIGN)
            nc.vector.tensor_copy(tile[:], hid[:, :, first : first + HALF].rearrange("p t o -> p o t"))
            grouped.append(tile)

        out_view = out.rearrange("(b p) o -> p b o", p=P)
        for h in range(2):
            codes = keep.tile([P, HALF], U32, name=f"hid_words{h}", align_bytes=ALIGN)
            scales = keep.tile([P, HALF], U8, name=f"hid_plane{h}", align_bytes=ALIGN)
            nc.vector.quantize_mx(out=codes[:].bitcast(FP8X4), scales=scales[:],
                                  in_=grouped[h][:].rearrange("p o t -> p (o t)"))
            for block in range(N // P):
                rows = slice(block * P, (block + 1) * P)
                y = psum.tile([P, HALF], F32, name="y")
                nc.tensor.matmul_mx(
                    out=y[:], lhsT=vg_words[:, rows].bitcast(FP4X4), lhsT_scale=vg_plane[:, rows],
                    rhs=codes[:].bitcast(FP8X4), rhs_scale=scales[:], start=True, stop=True,
                )
                y_sb = keep.tile([P, HALF], F32, name=f"y{h}{block}")
                if (h, block) == (1, 0):
                    nc.vector.tensor_copy(y_sb[:], y[:])
                else:
                    nc.scalar.copy(y_sb[:], y[:])
                queue = nc.scalar if (h, block) == (1, 1) else nc.sync
                queue.dma_start(out_view[:, block, h * HALF : (h + 1) * HALF], y_sb[:])
